import numpy as np
import ml_dtypes


def mxq(x, axis, fmt="e4m3"):
    dtype, down = {"e4m3": (ml_dtypes.float8_e4m3fn, 7), "e5m2": (ml_dtypes.float8_e5m2, 14)}[fmt]
    v = np.moveaxis(np.asarray(x, np.float32).astype(ml_dtypes.bfloat16).astype(np.float64), axis, -1)
    blocks = v.reshape(v.shape[:-1] + (-1, 32))
    amax = np.abs(blocks).max(-1, keepdims=True)
    byte = np.maximum(np.where(amax > 0, np.frexp(amax)[1] - 1 + 127, 0) - down, 1)
    scale = np.exp2(byte - 127.0)
    codes = (blocks / scale).astype(np.float32).astype(dtype).astype(np.float64)
    return np.moveaxis((codes * scale).reshape(v.shape), -1, axis)


WIDE = False


def mx_kscale(k, group=512):
    if not WIDE:
        return np.ones(k)
    levels = np.array([18, -18])
    if group != 512:
        return np.exp2(np.random.permutation(np.resize(levels, k // group))).repeat(group)
    if k % 512:
        return np.exp2(np.random.permutation(np.resize(levels, k // 32))).repeat(32)
    a = np.empty((k // 512, 16))
    for p in range(k // 512):
        a[p, :8] = np.random.permutation(np.resize(levels, 8))
        for g in range(8):
            far = levels[np.abs(levels - a[p, g]) >= 10]
            a[p, g + 8] = far[np.random.randint(len(far))]
    return np.exp2(a.ravel()).repeat(32)


def f64(x):
    return np.asarray(x).astype(np.float64)


H, D, N = 8, 128, 512


def setup_inputs():
    n = np.random.standard_normal
    s = mx_kscale(D, 0)[:, None]
    S = n((H, D, 128)) / np.sqrt(D)
    return {
        "q": n((H, D, N)).astype(np.float32),
        "qa": (np.random.uniform(0.5, 2.0, (D, 1)) * s).astype(np.float32),
        "S": (S / s).astype(np.float32),
    }


def reference(q, qa, S):
    fq = (1.0 / (1.0 + np.exp(-f64(q)))) * f64(qa)
    y = mxq(fq, 1, "e4m3").transpose(0, 2, 1) @ mxq(f64(S), 1, "e4m3")
    return y

@@ -1,0 +1,182 @@
+from contextlib import ExitStack
+
+import concourse.mybir as mybir
+
+F32 = mybir.dt.float32
+BF16 = mybir.dt.bfloat16
+U32 = mybir.dt.uint32
+U8 = mybir.dt.uint8
+FP8X4 = mybir.dt.float8_e4m3fn_x4
+SIGMOID = mybir.ActivationFunctionType.Sigmoid
+MULT = mybir.AluOpType.mult
+
+H, D, N, E = 8, 128, 512, 128
+FLOPS = 2 * H * N * D * E
+
+P = 128
+PACK = 4
+ROWS = D // PACK
+SIDE = P // ROWS
+SETS = H // SIDE
+M = 128
+R = 2
+TOK = M * R
+HALVES = N // TOK
+UNITS = SETS * HALVES
+PIECES = 2
+PTOK = TOK // PIECES
+PM = M // PIECES
+
+
+def tile_rows_read_sig_kernel(tc, q, qa, S, out):
+    nc = tc.nc
+    q_v = q.rearrange("(s c) (p j) n -> s (c p) j n", c=SIDE, j=PACK)
+    s_v = S.rearrange("(s c) (p j) e -> s (c p) j e", c=SIDE, j=PACK)
+    out_v = out.rearrange("h (u m r) e -> u m h (r e)", m=M, r=R)
+
+    with ExitStack() as ctx:
+        sb = ctx.enter_context(tc.tile_pool(name="sb", bufs=1))
+        ps = ctx.enter_context(tc.psum_pool(name="ps", bufs=1))
+        ctx.enter_context(tc.manual_schedule())
+
+        weights = sb.tile([P, PACK], F32, name="weights")
+        q_raw = [sb.tile([P, PACK, TOK], F32, name="q_raw%d" % u) for u in range(UNITS)]
+        s_raw = [sb.tile([P, PACK, E], F32, name="s_raw%d" % s) for s in range(SETS)]
+        phi = [[sb.tile([P, PTOK, PACK], F32, name="phi%d_%d" % (u, i)) for i in range(PIECES)] for u in range(UNITS)]
+        q_bf = [sb.tile([P, R, M, PACK], BF16, name="q_bf%d" % u, align_bytes=64) for u in range(UNITS)]
+        q_codes = [sb.tile([P, TOK], U32, name="q_codes%d" % u, align_bytes=64) for u in range(UNITS)]
+        q_scales = [sb.tile([P, TOK], U8, name="q_scales%d" % u, align_bytes=64) for u in range(UNITS)]
+        s_bf = [sb.tile([P, E, PACK], BF16, name="s_bf%d" % s, align_bytes=64) for s in range(SETS)]
+        s_codes = [sb.tile([P, E], U32, name="s_codes%d" % s, align_bytes=64) for s in range(SETS)]
+        s_scales = [sb.tile([P, E], U8, name="s_scales%d" % s, align_bytes=64) for s in range(SETS)]
+        res = [[sb.tile([P, 2, R * E], F32, name="res%d_%d" % (u, g)) for g in range(2)] for u in range(UNITS)]
+        banks = [[ps.tile([P, 512], F32, name="bank%d_%d" % (c, b)) for b in range(2)] for c in range(SIDE)]
+
+        def load_q(u):
+            s, half = divmod(u, HALVES)
+            nc.sync.dma_start(out=q_raw[u][:], in_=q_v[s, :, :, half * TOK : (half + 1) * TOK])
+
+        def load_s(s):
+            nc.sync.dma_start(out=s_raw[s][:], in_=s_v[s])
+
+        def sigmoid(u, i):
+            src = q_raw[u][:, :, i * PTOK : (i + 1) * PTOK]
+            nc.scalar.activation(
+                out=phi[u][i][:].rearrange("p (c i) j -> p c j i", i=4),
+                in_=src.rearrange("p j (c i) -> p c j i", i=4),
+                func=SIGMOID,
+            )
+
+        def weigh(u, i):
+            nc.vector.tensor_tensor(
+                out=q_bf[u][:, :, i * PM : (i + 1) * PM, :],
+                in0=phi[u][i][:].rearrange("p (m r) j -> p r m j", r=R),
+                in1=weights[:].unsqueeze(1).unsqueeze(1).to_broadcast([P, R, PM, PACK]),
+                op=MULT,
+            )
+
+        def quantise_q(u):
+            nc.vector.quantize_mx(
+                out=q_codes[u][:].bitcast(FP8X4),
+                scales=q_scales[u][:],
+                in_=q_bf[u][:].rearrange("p r m j -> p (r m j)"),
+            )
+
+        def round_s(s):
+            nc.vector.tensor_copy(
+                out=s_bf[s][:].rearrange("p (c i) j -> p c j i", i=4),
+                in_=s_raw[s][:].rearrange("p j (c i) -> p c j i", i=4),
+            )
+
+        def quantise_s(s):
+            nc.vector.quantize_mx(
+                out=s_codes[s][:].bitcast(FP8X4),
+                scales=s_scales[s][:],
+                in_=s_bf[s][:].rearrange("p e j -> p (e j)"),
+            )
+
+        def multiply(u):
+            s = u // HALVES
+            for r in range(R):
+                for c in range(SIDE):
+                    rows = slice(ROWS * c, ROWS * (c + 1))
+                    cols = slice(M * r, M * (r + 1))
+                    nc.tensor.matmul_mx(
+                        out=banks[c][u % 2][:, E * r : E * (r + 1)],
+                        lhsT=q_codes[u][rows, cols].bitcast(FP8X4),
+                        lhsT_scale=q_scales[u][rows, cols],
+                        rhs=s_codes[s][rows, :].bitcast(FP8X4),
+                        rhs_scale=s_scales[s][rows, :],
+                        start=True,
+                        stop=True,
+                    )
+
+        def empty(u, c, on_vector):
+            dst = res[u][c // 2][:, c % 2, :]
+            src = banks[c][u % 2][:, 0 : R * E]
+            if on_vector:
+                nc.vector.tensor_copy(out=dst, in_=src)
+            else:
+                nc.scalar.copy(out=dst, in_=src)
+
+        def store(u, g):
+            s, half = divmod(u, HALVES)
+            h0 = SIDE * s + 2 * g
+            nc.sync.dma_start(out=out_v[half, :, h0 : h0 + 2, :], in_=res[u][g][:])
+
+        nc.scalar.dma_start(out=weights[:], in_=qa.rearrange("d o -> (d o)").partition_broadcast(SIDE))
+        load_q(0)
+        load_s(0)
+        load_q(1)
+        load_q(2)
+        load_s(1)
+        load_q(3)
+
+        sigmoid(0, 0)
+        sigmoid(0, 1)
+        weigh(0, 0)
+        round_s(0)
+        weigh(0, 1)
+        quantise_s(0)
+        quantise_q(0)
+        multiply(0)
+        sigmoid(1, 0)
+        sigmoid(1, 1)
+        weigh(1, 0)
+        empty(0, 0, True)
+        weigh(1, 1)
+        empty(0, 1, True)
+        store(0, 0)
+        quantise_q(1)
+        multiply(1)
+        empty(0, 2, False)
+        empty(0, 3, False)
+        store(0, 1)
+        sigmoid(2, 0)
+        sigmoid(2, 1)
+        round_s(1)
+        weigh(2, 0)
+        quantise_s(1)
+        weigh(2, 1)
+        for g in range(2):
+            empty(1, 2 * g, False)
+            empty(1, 2 * g + 1, False)
+            store(1, g)
+        sigmoid(3, 0)
+        sigmoid(3, 1)
+        quantise_q(2)
+        multiply(2)
+        weigh(3, 0)
+        weigh(3, 1)
+        for g in range(2):
+            empty(2, 2 * g, False)
+            empty(2, 2 * g + 1, False)
+            store(2, g)
+        quantise_q(3)
+        multiply(3)
+        empty(3, 0, True)
+        empty(3, 1, True)
+        store(3, 0)
+        empty(3, 2, False)
+        empty(3, 3, False)
+        store(3, 1)

@@ -126,57 +126,60 @@ def tile_rows_read_sig_kernel(tc, q, qa, S, out):
 
         nc.scalar.dma_start(out=weights[:], in_=qa.rearrange("d o -> (d o)").partition_broadcast(SIDE))
         load_q(0)
-        load_s(0)
         load_q(1)
+        load_s(0)
         load_q(2)
         load_s(1)
         load_q(3)
-
         sigmoid(0, 0)
         sigmoid(0, 1)
         weigh(0, 0)
-        round_s(0)
         weigh(0, 1)
-        quantise_s(0)
+        round_s(0)
         quantise_q(0)
+        quantise_s(0)
         multiply(0)
         sigmoid(1, 0)
         sigmoid(1, 1)
         weigh(1, 0)
-        empty(0, 0, True)
         weigh(1, 1)
-        empty(0, 1, True)
-        store(0, 0)
+        round_s(1)
         quantise_q(1)
+        quantise_s(1)
         multiply(1)
+        sigmoid(2, 0)
+        sigmoid(2, 1)
+        weigh(2, 0)
+        weigh(2, 1)
+        empty(0, 0, False)
+        empty(0, 1, False)
+        store(0, 0)
         empty(0, 2, False)
         empty(0, 3, False)
         store(0, 1)
-        sigmoid(2, 0)
-        sigmoid(2, 1)
-        round_s(1)
-        weigh(2, 0)
-        quantise_s(1)
-        weigh(2, 1)
-        for g in range(2):
-            empty(1, 2 * g, False)
-            empty(1, 2 * g + 1, False)
-            store(1, g)
-        sigmoid(3, 0)
-        sigmoid(3, 1)
+        empty(1, 0, True)
         quantise_q(2)
         multiply(2)
+        empty(1, 1, True)
+        store(1, 0)
+        sigmoid(3, 0)
+        sigmoid(3, 1)
         weigh(3, 0)
         weigh(3, 1)
-        for g in range(2):
-            empty(2, 2 * g, False)
-            empty(2, 2 * g + 1, False)
-            store(2, g)
+        empty(1, 2, False)
+        empty(1, 3, False)
+        store(1, 1)
+        empty(2, 0, False)
+        empty(2, 1, False)
+        store(2, 0)
         quantise_q(3)
         multiply(3)
-        empty(3, 0, True)
-        empty(3, 1, True)
+        empty(2, 2, True)
+        empty(2, 3, True)
+        store(2, 1)
+        empty(3, 0, False)
+        empty(3, 1, False)
         store(3, 0)
-        empty(3, 2, False)
-        empty(3, 3, False)
+        empty(3, 2, True)
+        empty(3, 3, True)
         store(3, 1)

@@ -23,9 +23,7 @@ R = 2
 TOK = M * R
 HALVES = N // TOK
 UNITS = SETS * HALVES
-PIECES = 2
-PTOK = TOK // PIECES
-PM = M // PIECES
+PAIR = 2
 
 
 def tile_rows_read_sig_kernel(tc, q, qa, S, out):
@@ -42,10 +40,11 @@ def tile_rows_read_sig_kernel(tc, q, qa, S, out):
         weights = sb.tile([P, PACK], F32, name="weights")
         q_raw = [sb.tile([P, PACK, TOK], F32, name="q_raw%d" % u) for u in range(UNITS)]
         s_raw = [sb.tile([P, PACK, E], F32, name="s_raw%d" % s) for s in range(SETS)]
-        phi = [[sb.tile([P, PTOK, PACK], F32, name="phi%d_%d" % (u, i)) for i in range(PIECES)] for u in range(UNITS)]
-        q_bf = [sb.tile([P, R, M, PACK], BF16, name="q_bf%d" % u, align_bytes=64) for u in range(UNITS)]
-        q_codes = [sb.tile([P, TOK], U32, name="q_codes%d" % u, align_bytes=64) for u in range(UNITS)]
-        q_scales = [sb.tile([P, TOK], U8, name="q_scales%d" % u, align_bytes=64) for u in range(UNITS)]
+        weight_pairs = sb.tile([P, PACK, PAIR], F32, name="weight_pairs")
+        phi = [[sb.tile([P, PACK, M], F32, name="phi%d_%d" % (u, r)) for r in range(R)] for u in range(UNITS)]
+        q_bf = [[sb.tile([P, M, PACK], BF16, name="q_bf%d_%d" % (u, r), align_bytes=64) for r in range(R)] for u in range(UNITS)]
+        q_codes = [[sb.tile([P, M], U32, name="q_codes%d_%d" % (u, r), align_bytes=64) for r in range(R)] for u in range(UNITS)]
+        q_scales = [[sb.tile([P, M], U8, name="q_scales%d_%d" % (u, r), align_bytes=64) for r in range(R)] for u in range(UNITS)]
         s_bf = [sb.tile([P, E, PACK], BF16, name="s_bf%d" % s, align_bytes=64) for s in range(SETS)]
         s_codes = [sb.tile([P, E], U32, name="s_codes%d" % s, align_bytes=64) for s in range(SETS)]
         s_scales = [sb.tile([P, E], U8, name="s_scales%d" % s, align_bytes=64) for s in range(SETS)]
@@ -59,27 +58,33 @@ def tile_rows_read_sig_kernel(tc, q, qa, S, out):
         def load_s(s):
             nc.sync.dma_start(out=s_raw[s][:], in_=s_v[s])
 
-        def sigmoid(u, i):
-            src = q_raw[u][:, :, i * PTOK : (i + 1) * PTOK]
+        def load_weights():
+            for c in range(SIDE):
+                nc.sync.dma_start(out=weights[ROWS * c : ROWS * (c + 1), :], in_=qa.rearrange("(p j) o -> p (j o)", j=PACK))
+
+        def sigmoid(u, r):
             nc.scalar.activation(
-                out=phi[u][i][:].rearrange("p (c i) j -> p c j i", i=4),
-                in_=src.rearrange("p j (c i) -> p c j i", i=4),
+                out=phi[u][r][:],
+                in_=q_raw[u][:].rearrange("p j (m r) -> p r j m", r=R)[:, r, :, :],
                 func=SIGMOID,
             )
 
-        def weigh(u, i):
+        def pair_weights():
+            nc.vector.tensor_copy(out=weight_pairs[:], in_=weights[:].unsqueeze(2).to_broadcast([P, PACK, PAIR]))
+
+        def weigh(u, r):
             nc.vector.tensor_tensor(
-                out=q_bf[u][:, :, i * PM : (i + 1) * PM, :],
-                in0=phi[u][i][:].rearrange("p (m r) j -> p r m j", r=R),
-                in1=weights[:].unsqueeze(1).unsqueeze(1).to_broadcast([P, R, PM, PACK]),
+                out=q_bf[u][r][:].rearrange("p (c i) j -> p c j i", i=PAIR),
+                in0=phi[u][r][:].rearrange("p j (c i) -> p c j i", i=PAIR),
+                in1=weight_pairs[:].unsqueeze(1).to_broadcast([P, M // PAIR, PACK, PAIR]),
                 op=MULT,
             )
 
-        def quantise_q(u):
+        def quantise_q(u, r):
             nc.vector.quantize_mx(
-                out=q_codes[u][:].bitcast(FP8X4),
-                scales=q_scales[u][:],
-                in_=q_bf[u][:].rearrange("p r m j -> p (r m j)"),
+                out=q_codes[u][r][:].bitcast(FP8X4),
+                scales=q_scales[u][r][:],
+                in_=q_bf[u][r][:].rearrange("p m j -> p (m j)"),
             )
 
         def round_s(s):
@@ -95,21 +100,19 @@ def tile_rows_read_sig_kernel(tc, q, qa, S, out):
                 in_=s_bf[s][:].rearrange("p e j -> p (e j)"),
             )
 
-        def multiply(u):
+        def multiply(u, r):
             s = u // HALVES
-            for r in range(R):
-                for c in range(SIDE):
-                    rows = slice(ROWS * c, ROWS * (c + 1))
-                    cols = slice(M * r, M * (r + 1))
-                    nc.tensor.matmul_mx(
-                        out=banks[c][u % 2][:, E * r : E * (r + 1)],
-                        lhsT=q_codes[u][rows, cols].bitcast(FP8X4),
-                        lhsT_scale=q_scales[u][rows, cols],
-                        rhs=s_codes[s][rows, :].bitcast(FP8X4),
-                        rhs_scale=s_scales[s][rows, :],
-                        start=True,
-                        stop=True,
-                    )
+            for c in range(SIDE):
+                rows = slice(ROWS * c, ROWS * (c + 1))
+                nc.tensor.matmul_mx(
+                    out=banks[c][u % 2][:, E * r : E * (r + 1)],
+                    lhsT=q_codes[u][r][rows, :].bitcast(FP8X4),
+                    lhsT_scale=q_scales[u][r][rows, :],
+                    rhs=s_codes[s][rows, :].bitcast(FP8X4),
+                    rhs_scale=s_scales[s][rows, :],
+                    start=True,
+                    stop=True,
+                )
 
         def empty(u, c, on_vector):
             dst = res[u][c // 2][:, c % 2, :]
@@ -124,29 +127,34 @@ def tile_rows_read_sig_kernel(tc, q, qa, S, out):
             h0 = SIDE * s + 2 * g
             nc.sync.dma_start(out=out_v[half, :, h0 : h0 + 2, :], in_=res[u][g][:])
 
-        nc.scalar.dma_start(out=weights[:], in_=qa.rearrange("d o -> (d o)").partition_broadcast(SIDE))
         load_q(0)
+        load_weights()
         load_q(1)
         load_s(0)
         load_q(2)
         load_s(1)
         load_q(3)
+        pair_weights()
         sigmoid(0, 0)
         sigmoid(0, 1)
         weigh(0, 0)
         weigh(0, 1)
         round_s(0)
-        quantise_q(0)
+        quantise_q(0, 0)
+        quantise_q(0, 1)
         quantise_s(0)
-        multiply(0)
+        multiply(0, 0)
+        multiply(0, 1)
         sigmoid(1, 0)
         sigmoid(1, 1)
         weigh(1, 0)
         weigh(1, 1)
         round_s(1)
-        quantise_q(1)
+        quantise_q(1, 0)
+        quantise_q(1, 1)
         quantise_s(1)
-        multiply(1)
+        multiply(1, 0)
+        multiply(1, 1)
         sigmoid(2, 0)
         sigmoid(2, 1)
         weigh(2, 0)
@@ -158,8 +166,10 @@ def tile_rows_read_sig_kernel(tc, q, qa, S, out):
         empty(0, 3, False)
         store(0, 1)
         empty(1, 0, True)
-        quantise_q(2)
-        multiply(2)
+        quantise_q(2, 0)
+        quantise_q(2, 1)
+        multiply(2, 0)
+        multiply(2, 1)
         empty(1, 1, True)
         store(1, 0)
         sigmoid(3, 0)
@@ -172,8 +182,10 @@ def tile_rows_read_sig_kernel(tc, q, qa, S, out):
         empty(2, 0, False)
         empty(2, 1, False)
         store(2, 0)
-        quantise_q(3)
-        multiply(3)
+        quantise_q(3, 0)
+        multiply(3, 0)
+        quantise_q(3, 1)
+        multiply(3, 1)
         empty(2, 2, True)
         empty(2, 3, True)
         store(2, 1)

@@ -24,13 +24,16 @@ TOK = M * R
 HALVES = N // TOK
 UNITS = SETS * HALVES
 PAIR = 2
+RUN = 4
+BANK = 512
 
 
 def tile_rows_read_sig_kernel(tc, q, qa, S, out):
     nc = tc.nc
     q_v = q.rearrange("(s c) (p j) n -> s (c p) j n", c=SIDE, j=PACK)
     s_v = S.rearrange("(s c) (p j) e -> s (c p) j e", c=SIDE, j=PACK)
-    out_v = out.rearrange("h (u m r) e -> u m h (r e)", m=M, r=R)
+    qa_v = qa.rearrange("(p j) o -> p (j o)", j=PACK)
+    out_v = out.rearrange("h (half m r) e -> h half m (r e)", m=M, r=R)
 
     with ExitStack() as ctx:
         sb = ctx.enter_context(tc.tile_pool(name="sb", bufs=1))
@@ -38,9 +41,9 @@ def tile_rows_read_sig_kernel(tc, q, qa, S, out):
         ctx.enter_context(tc.manual_schedule())
 
         weights = sb.tile([P, PACK], F32, name="weights")
+        weight_pairs = sb.tile([P, PACK, PAIR], F32, name="weight_pairs")
         q_raw = [sb.tile([P, PACK, TOK], F32, name="q_raw%d" % u) for u in range(UNITS)]
         s_raw = [sb.tile([P, PACK, E], F32, name="s_raw%d" % s) for s in range(SETS)]
-        weight_pairs = sb.tile([P, PACK, PAIR], F32, name="weight_pairs")
         phi = [[sb.tile([P, PACK, M], F32, name="phi%d_%d" % (u, r)) for r in range(R)] for u in range(UNITS)]
         q_bf = [[sb.tile([P, M, PACK], BF16, name="q_bf%d_%d" % (u, r), align_bytes=64) for r in range(R)] for u in range(UNITS)]
         q_codes = [[sb.tile([P, M], U32, name="q_codes%d_%d" % (u, r), align_bytes=64) for r in range(R)] for u in range(UNITS)]
@@ -48,8 +51,8 @@ def tile_rows_read_sig_kernel(tc, q, qa, S, out):
         s_bf = [sb.tile([P, E, PACK], BF16, name="s_bf%d" % s, align_bytes=64) for s in range(SETS)]
         s_codes = [sb.tile([P, E], U32, name="s_codes%d" % s, align_bytes=64) for s in range(SETS)]
         s_scales = [sb.tile([P, E], U8, name="s_scales%d" % s, align_bytes=64) for s in range(SETS)]
-        res = [[sb.tile([P, 2, R * E], F32, name="res%d_%d" % (u, g)) for g in range(2)] for u in range(UNITS)]
-        banks = [[ps.tile([P, 512], F32, name="bank%d_%d" % (c, b)) for b in range(2)] for c in range(SIDE)]
+        res = [[sb.tile([P, R * E], F32, name="res%d_%d" % (u, c)) for c in range(SIDE)] for u in range(UNITS)]
+        banks = [[ps.tile([P, BANK], F32, name="bank%d_%d" % (c, parity)) for parity in range(2)] for c in range(SIDE)]
 
         def load_q(u):
             s, half = divmod(u, HALVES)
@@ -60,25 +63,25 @@ def tile_rows_read_sig_kernel(tc, q, qa, S, out):
 
         def load_weights():
             for c in range(SIDE):
-                nc.sync.dma_start(out=weights[ROWS * c : ROWS * (c + 1), :], in_=qa.rearrange("(p j) o -> p (j o)", j=PACK))
-
-        def sigmoid(u, r):
-            nc.scalar.activation(
-                out=phi[u][r][:],
-                in_=q_raw[u][:].rearrange("p j (m r) -> p r j m", r=R)[:, r, :, :],
-                func=SIGMOID,
-            )
+                nc.sync.dma_start(out=weights[ROWS * c : ROWS * (c + 1), :], in_=qa_v)
 
         def pair_weights():
             nc.vector.tensor_copy(out=weight_pairs[:], in_=weights[:].unsqueeze(2).to_broadcast([P, PACK, PAIR]))
 
-        def weigh(u, r):
-            nc.vector.tensor_tensor(
-                out=q_bf[u][r][:].rearrange("p (c i) j -> p c j i", i=PAIR),
-                in0=phi[u][r][:].rearrange("p j (c i) -> p c j i", i=PAIR),
-                in1=weight_pairs[:].unsqueeze(1).to_broadcast([P, M // PAIR, PACK, PAIR]),
-                op=MULT,
-            )
+        def map_and_weigh(u):
+            for r in range(R):
+                nc.scalar.activation(
+                    out=phi[u][r][:],
+                    in_=q_raw[u][:].rearrange("p j (m r) -> p r j m", r=R)[:, r, :, :],
+                    func=SIGMOID,
+                )
+            for r in range(R):
+                nc.vector.tensor_tensor(
+                    out=q_bf[u][r][:].rearrange("p (c i) j -> p c j i", i=PAIR),
+                    in0=phi[u][r][:].rearrange("p j (c i) -> p c j i", i=PAIR),
+                    in1=weight_pairs[:].unsqueeze(1).to_broadcast([P, M // PAIR, PACK, PAIR]),
+                    op=MULT,
+                )
 
         def quantise_q(u, r):
             nc.vector.quantize_mx(
@@ -89,8 +92,8 @@ def tile_rows_read_sig_kernel(tc, q, qa, S, out):
 
         def round_s(s):
             nc.vector.tensor_copy(
-                out=s_bf[s][:].rearrange("p (c i) j -> p c j i", i=4),
-                in_=s_raw[s][:].rearrange("p j (c i) -> p c j i", i=4),
+                out=s_bf[s][:].rearrange("p (c i) j -> p c j i", i=RUN),
+                in_=s_raw[s][:].rearrange("p j (c i) -> p c j i", i=RUN),
             )
 
         def quantise_s(s):
@@ -114,18 +117,13 @@ def tile_rows_read_sig_kernel(tc, q, qa, S, out):
                     stop=True,
                 )
 
-        def empty(u, c, on_vector):
-            dst = res[u][c // 2][:, c % 2, :]
-            src = banks[c][u % 2][:, 0 : R * E]
-            if on_vector:
-                nc.vector.tensor_copy(out=dst, in_=src)
-            else:
-                nc.scalar.copy(out=dst, in_=src)
-
-        def store(u, g):
+        def hand_out(u, c, copy):
             s, half = divmod(u, HALVES)
-            h0 = SIDE * s + 2 * g
-            nc.sync.dma_start(out=out_v[half, :, h0 : h0 + 2, :], in_=res[u][g][:])
+            copy(out=res[u][c][:], in_=banks[c][u % 2][:, 0 : R * E])
+            nc.sync.dma_start(out=out_v[SIDE * s + c, half], in_=res[u][c][:])
+
+        on_scalar = nc.scalar.copy
+        on_vector = nc.vector.tensor_copy
 
         load_q(0)
         load_weights()
@@ -135,63 +133,35 @@ def tile_rows_read_sig_kernel(tc, q, qa, S, out):
         load_s(1)
         load_q(3)
         pair_weights()
-        sigmoid(0, 0)
-        sigmoid(0, 1)
-        weigh(0, 0)
-        weigh(0, 1)
-        round_s(0)
-        quantise_q(0, 0)
-        quantise_q(0, 1)
-        quantise_s(0)
-        multiply(0, 0)
-        multiply(0, 1)
-        sigmoid(1, 0)
-        sigmoid(1, 1)
-        weigh(1, 0)
-        weigh(1, 1)
-        round_s(1)
-        quantise_q(1, 0)
-        quantise_q(1, 1)
-        quantise_s(1)
-        multiply(1, 0)
-        multiply(1, 1)
-        sigmoid(2, 0)
-        sigmoid(2, 1)
-        weigh(2, 0)
-        weigh(2, 1)
-        empty(0, 0, False)
-        empty(0, 1, False)
-        store(0, 0)
-        empty(0, 2, False)
-        empty(0, 3, False)
-        store(0, 1)
-        empty(1, 0, True)
-        quantise_q(2, 0)
-        quantise_q(2, 1)
-        multiply(2, 0)
-        multiply(2, 1)
-        empty(1, 1, True)
-        store(1, 0)
-        sigmoid(3, 0)
-        sigmoid(3, 1)
-        weigh(3, 0)
-        weigh(3, 1)
-        empty(1, 2, False)
-        empty(1, 3, False)
-        store(1, 1)
-        empty(2, 0, False)
-        empty(2, 1, False)
-        store(2, 0)
-        quantise_q(3, 0)
-        multiply(3, 0)
-        quantise_q(3, 1)
-        multiply(3, 1)
-        empty(2, 2, True)
-        empty(2, 3, True)
-        store(2, 1)
-        empty(3, 0, False)
-        empty(3, 1, False)
-        store(3, 0)
-        empty(3, 2, True)
-        empty(3, 3, True)
-        store(3, 1)
+
+        for u in range(SETS):
+            map_and_weigh(u)
+            round_s(u)
+            for r in range(R):
+                quantise_q(u, r)
+            quantise_s(u)
+            for r in range(R):
+                multiply(u, r)
+
+        map_and_weigh(2)
+        for c in range(SIDE):
+            hand_out(0, c, on_scalar)
+        hand_out(1, 0, on_vector)
+        for r in range(R):
+            quantise_q(2, r)
+        for r in range(R):
+            multiply(2, r)
+        hand_out(1, 1, on_vector)
+
+        map_and_weigh(3)
+        for u, c in ((1, 2), (1, 3), (2, 0), (2, 1)):
+            hand_out(u, c, on_scalar)
+        for r in range(R):
+            quantise_q(3, r)
+            multiply(3, r)
+        for c in (2, 3):
+            hand_out(2, c, on_vector)
+
+        for c in range(SIDE // 2):
+            hand_out(3, c, on_scalar)
+            hand_out(3, c + SIDE // 2, on_vector)

from contextlib import ExitStack

import concourse.mybir as mybir

F32 = mybir.dt.float32
BF16 = mybir.dt.bfloat16
U32 = mybir.dt.uint32
U8 = mybir.dt.uint8
FP8X4 = mybir.dt.float8_e4m3fn_x4
SIGMOID = mybir.ActivationFunctionType.Sigmoid
MULT = mybir.AluOpType.mult

H, D, N, E = 8, 128, 512, 128
FLOPS = 2 * H * N * D * E

P = 128
PACK = 4
ROWS = D // PACK
SIDE = P // ROWS
SETS = H // SIDE
M = 128
R = 2
TOK = M * R
HALVES = N // TOK
UNITS = SETS * HALVES
PAIR = 2
RUN = 4
BANK = 512


def tile_rows_read_sig_kernel(tc, q, qa, S, out):
    nc = tc.nc
    q_v = q.rearrange("(s c) (p j) n -> s (c p) j n", c=SIDE, j=PACK)
    s_v = S.rearrange("(s c) (p j) e -> s (c p) j e", c=SIDE, j=PACK)
    qa_v = qa.rearrange("(p j) o -> p (j o)", j=PACK)
    out_v = out.rearrange("h (half m r) e -> h half m (r e)", m=M, r=R)

    with ExitStack() as ctx:
        sb = ctx.enter_context(tc.tile_pool(name="sb", bufs=1))
        ps = ctx.enter_context(tc.psum_pool(name="ps", bufs=1))
        ctx.enter_context(tc.manual_schedule())

        weights = sb.tile([P, PACK], F32, name="weights")
        weight_pairs = sb.tile([P, PACK, PAIR], F32, name="weight_pairs")
        q_raw = [sb.tile([P, PACK, TOK], F32, name="q_raw%d" % u) for u in range(UNITS)]
        s_raw = [sb.tile([P, PACK, E], F32, name="s_raw%d" % s) for s in range(SETS)]
        phi = [[sb.tile([P, PACK, M], F32, name="phi%d_%d" % (u, r)) for r in range(R)] for u in range(UNITS)]
        q_bf = [[sb.tile([P, M, PACK], BF16, name="q_bf%d_%d" % (u, r), align_bytes=64) for r in range(R)] for u in range(UNITS)]
        q_codes = [[sb.tile([P, M], U32, name="q_codes%d_%d" % (u, r), align_bytes=64) for r in range(R)] for u in range(UNITS)]
        q_scales = [[sb.tile([P, M], U8, name="q_scales%d_%d" % (u, r), align_bytes=64) for r in range(R)] for u in range(UNITS)]
        s_bf = [sb.tile([P, E, PACK], BF16, name="s_bf%d" % s, align_bytes=64) for s in range(SETS)]
        s_codes = [sb.tile([P, E], U32, name="s_codes%d" % s, align_bytes=64) for s in range(SETS)]
        s_scales = [sb.tile([P, E], U8, name="s_scales%d" % s, align_bytes=64) for s in range(SETS)]
        res = [[sb.tile([P, R * E], F32, name="res%d_%d" % (u, c)) for c in range(SIDE)] for u in range(UNITS)]
        banks = [[ps.tile([P, BANK], F32, name="bank%d_%d" % (c, parity)) for parity in range(2)] for c in range(SIDE)]

        def load_q(u):
            s, half = divmod(u, HALVES)
            nc.sync.dma_start(out=q_raw[u][:], in_=q_v[s, :, :, half * TOK : (half + 1) * TOK])

        def load_s(s):
            nc.sync.dma_start(out=s_raw[s][:], in_=s_v[s])

        def load_weights():
            for c in range(SIDE):
                nc.sync.dma_start(out=weights[ROWS * c : ROWS * (c + 1), :], in_=qa_v)

        def pair_weights():
            nc.vector.tensor_copy(out=weight_pairs[:], in_=weights[:].unsqueeze(2).to_broadcast([P, PACK, PAIR]))

        def map_and_weigh(u):
            for r in range(R):
                nc.scalar.activation(
                    out=phi[u][r][:],
                    in_=q_raw[u][:].rearrange("p j (m r) -> p r j m", r=R)[:, r, :, :],
                    func=SIGMOID,
                )
            for r in range(R):
                nc.vector.tensor_tensor(
                    out=q_bf[u][r][:].rearrange("p (c i) j -> p c j i", i=PAIR),
                    in0=phi[u][r][:].rearrange("p j (c i) -> p c j i", i=PAIR),
                    in1=weight_pairs[:].unsqueeze(1).to_broadcast([P, M // PAIR, PACK, PAIR]),
                    op=MULT,
                )

        def quantise_q(u, r):
            nc.vector.quantize_mx(
                out=q_codes[u][r][:].bitcast(FP8X4),
                scales=q_scales[u][r][:],
                in_=q_bf[u][r][:].rearrange("p m j -> p (m j)"),
            )

        def round_s(s):
            nc.vector.tensor_copy(
                out=s_bf[s][:].rearrange("p (c i) j -> p c j i", i=RUN),
                in_=s_raw[s][:].rearrange("p j (c i) -> p c j i", i=RUN),
            )

        def quantise_s(s):
            nc.vector.quantize_mx(
                out=s_codes[s][:].bitcast(FP8X4),
                scales=s_scales[s][:],
                in_=s_bf[s][:].rearrange("p e j -> p (e j)"),
            )

        def multiply(u, r):
            s = u // HALVES
            for c in range(SIDE):
                rows = slice(ROWS * c, ROWS * (c + 1))
                nc.tensor.matmul_mx(
                    out=banks[c][u % 2][:, E * r : E * (r + 1)],
                    lhsT=q_codes[u][r][rows, :].bitcast(FP8X4),
                    lhsT_scale=q_scales[u][r][rows, :],
                    rhs=s_codes[s][rows, :].bitcast(FP8X4),
                    rhs_scale=s_scales[s][rows, :],
                    start=True,
                    stop=True,
                )

        def hand_out(u, c, copy):
            s, half = divmod(u, HALVES)
            copy(out=res[u][c][:], in_=banks[c][u % 2][:, 0 : R * E])
            nc.sync.dma_start(out=out_v[SIDE * s + c, half], in_=res[u][c][:])

        on_scalar = nc.scalar.copy
        on_vector = nc.vector.tensor_copy

        load_q(0)
        load_weights()
        load_q(1)
        load_s(0)
        load_q(2)
        load_s(1)
        load_q(3)
        pair_weights()

        for u in range(SETS):
            map_and_weigh(u)
            round_s(u)
            for r in range(R):
                quantise_q(u, r)
            quantise_s(u)
            for r in range(R):
                multiply(u, r)

        map_and_weigh(2)
        for c in range(SIDE):
            hand_out(0, c, on_scalar)
        hand_out(1, 0, on_vector)
        for r in range(R):
            quantise_q(2, r)
        for r in range(R):
            multiply(2, r)
        hand_out(1, 1, on_vector)

        map_and_weigh(3)
        for u, c in ((1, 2), (1, 3), (2, 0), (2, 1)):
            hand_out(u, c, on_scalar)
        for r in range(R):
            quantise_q(3, r)
            multiply(3, r)
        for c in (2, 3):
            hand_out(2, c, on_vector)

        for c in range(SIDE // 2):
            hand_out(3, c, on_scalar)
            hand_out(3, c + SIDE // 2, on_vector)
